import numpy as np
import ml_dtypes


def mxq(x, axis, fmt="e4m3"):
    dtype, down = {"e4m3": (ml_dtypes.float8_e4m3fn, 7), "e5m2": (ml_dtypes.float8_e5m2, 14)}[fmt]
    v = np.moveaxis(np.asarray(x, np.float32).astype(ml_dtypes.bfloat16).astype(np.float64), axis, -1)
    blocks = v.reshape(v.shape[:-1] + (-1, 32))
    amax = np.abs(blocks).max(-1, keepdims=True)
    byte = np.maximum(np.where(amax > 0, np.frexp(amax)[1] - 1 + 127, 0) - down, 1)
    scale = np.exp2(byte - 127.0)
    codes = (blocks / scale).astype(np.float32).astype(dtype).astype(np.float64)
    return np.moveaxis((codes * scale).reshape(v.shape), -1, axis)


WIDE = False


def mx_kscale(k):
    if not WIDE:
        return np.ones(k)
    levels = np.array([10, -10, 5, -5, 0])
    if k % 512:
        return np.exp2(np.random.permutation(np.resize(levels, k // 32))).repeat(32)
    a = np.empty((k // 512, 16))
    for p in range(k // 512):
        a[p, :8] = np.random.permutation(np.resize(levels, 8))
        for g in range(8):
            far = levels[np.abs(levels - a[p, g]) >= 10]
            a[p, g + 8] = far[np.random.randint(len(far))]
    return np.exp2(a.ravel()).repeat(32)


def f64(x):
    return np.asarray(x).astype(np.float64)


def striped(idx):
    return np.tile(idx.reshape(-1, 16).T, (8, 1)).astype(np.uint16)


def unstriped(offs):
    return offs[:16].T.reshape(-1).astype(np.int64)


def pack_weight(w):
    k, n = w.shape
    w = f64(np.asarray(w, np.float32).astype(ml_dtypes.bfloat16)).reshape(k // 32, 32, n)
    amax = np.abs(w).max(1)
    byte = np.clip(np.where(amax > 0, np.frexp(amax)[1] - 1 + 127 - 7, 1), 1, 254)
    scaled = (w * np.exp2(127.0 - byte)[:, None, :]).reshape(k, n).astype(np.float32)
    words = np.ascontiguousarray(scaled.reshape(k // 512, 128, 4, n).transpose(0, 1, 3, 2)).astype(ml_dtypes.float8_e4m3fn).view(np.uint8)
    return words, np.ascontiguousarray(byte.astype(np.uint8).reshape(k // 512, 16, n))


def unpack_weight(words, scales):
    g, p, n, _ = words.shape
    vals = np.ascontiguousarray(words).view(ml_dtypes.float8_e4m3fn).astype(np.float64) * np.repeat(np.exp2(scales.astype(np.float64) - 127.0), 8, axis=1)[..., None]
    return vals.transpose(0, 1, 3, 2).reshape(g * 512, n)


K, T, S, V = 512, 2048, 512, 256


def setup_inputs():
    n = np.random.standard_normal
    s = mx_kscale(K)[:, None]
    packed_xT = pack_weight(n((K, T)) * s)
    return {
        "x_words": packed_xT[0],
        "x_scales": packed_xT[1],
        "hT": (n((K, V)) / np.sqrt(K) / s).astype(np.float32),
        "g1": ((np.random.uniform(size=(V, S)) < 0.5) * 1.0).astype(np.float32),
        "g2": ((np.random.uniform(size=(V, S)) < 0.5) * 1.0).astype(np.float32),
        "g3": ((np.random.uniform(size=(V, S)) < 0.5) * 1.0).astype(np.float32),
        "offs": striped(np.random.permutation(T)[:S]),
    }


def reference(x_words, x_scales, hT, g1, g2, g3, offs):
    hTq = mxq(f64(hT), 0, "e4m3")
    xq = unpack_weight(x_words, x_scales)[:, unstriped(offs)]
    y = hTq.T @ xq
    ex = np.exp(y - y.max(axis=1, keepdims=True))
    p0 = ex / ex.sum(axis=1, keepdims=True)
    r1 = p0 * f64(g1)
    t1 = r1.sum(axis=1, keepdims=True)
    p1 = p0 + r1 - (p0 * t1)
    r2 = p1 * f64(g2)
    t2 = r2.sum(axis=1, keepdims=True)
    p2 = p1 + r2 - (p1 * t2)
    r3 = p2 * f64(g3)
    t3 = r3.sum(axis=1, keepdims=True)
    p3 = p2 + r3 - (p2 * t3)
    return 512.0 * p3

@@ -1,0 +1,104 @@
+from contextlib import ExitStack
+
+import concourse.mybir as mybir
+
+K, T, S, V = 512, 2048, 512, 256
+FLOPS = 2 * K * S * V
+
+F32 = mybir.dt.float32
+BF16 = mybir.dt.bfloat16
+I32 = mybir.dt.int32
+U32 = mybir.dt.uint32
+U16 = mybir.dt.uint16
+U8 = mybir.dt.uint8
+FP8X4 = mybir.dt.float8_e4m3fn_x4
+ALU = mybir.AluOpType
+ACT = mybir.ActivationFunctionType
+AX = mybir.AxisListType
+
+P = 128
+PACK = 4
+TILES = V // P
+OUT_SCALE = 512.0
+
+
+def tile_picked_ysynth_three_p_kernel(tc, x_words, x_scales, hT, g1, g2, g3, offs, out):
+    nc = tc.nc
+    with ExitStack() as ctx:
+        sb = ctx.enter_context(tc.tile_pool(name="sb", bufs=1))
+        ps = ctx.enter_context(tc.psum_pool(name="ps", bufs=1))
+
+        offsets = sb.tile([P, S // 16], U16, name="offsets")
+        word_table = sb.tile([P, T], I32, name="word_table", align_bytes=64)
+        scale_table = sb.tile([P, T], U8, name="scale_table", tag="scale_then_code", align_bytes=64)
+        h_raw = sb.tile([P, PACK, V], F32, name="h_raw")
+        warm = sb.tile([P, 1], F32, name="warm", tag="warm_then_g")
+        warm_out = sb.tile([P, 1], F32, name="warm_out")
+
+        nc.vector.memset(scale_table[:].bitcast(I32), 0)
+        nc.vector.memset(warm[:], 0.0)
+
+        nc.sync.dma_start(offsets[:], offs)
+        nc.sync.dma_start(h_raw[:], hT.rearrange("(p j) t -> p j t", j=PACK))
+        nc.sync.dma_start(word_table[:], x_words[0].rearrange("p n t -> p (n t)").bitcast(I32))
+        for q in range(4):
+            nc.scalar.dma_start(scale_table[32 * q:32 * q + 4, :].bitcast(I32), x_scales[0, 4 * q:4 * q + 4, :].bitcast(I32))
+        nc.scalar.activation(warm_out[:], warm[:], ACT.Exp)
+        g_all = sb.tile([P, 3, TILES, S], F32, name="g_all", tag="warm_then_g")
+        g_sb = [g_all[:, r] for r in range(3)]
+        for r, g in enumerate((g1, g2, g3)):
+            nc.sync.dma_start(g_sb[r], g.rearrange("(a p) s -> p a s", p=P))
+
+        x_scale = sb.tile([P, S], U8, name="x_scale", align_bytes=64)
+        nc.vector.tensor_copy(x_scale[:], scale_table[:].indirect(offsets[:]))
+
+        h_bf = sb.tile([P, V * PACK], BF16, name="h_bf", align_bytes=64)
+        h_code = sb.tile([P, V], U32, name="h_code", align_bytes=64)
+        h_scale = sb.tile([P, V], U8, name="h_scale", align_bytes=64)
+        nc.scalar.copy(h_bf[:].rearrange("p (c i j) -> p c j i", i=4, j=PACK), h_raw[:].rearrange("p j (c i) -> p c j i", i=4))
+        nc.vector.quantize_mx(out=h_code[:].bitcast(FP8X4), scales=h_scale[:], in_=h_bf[:])
+
+        x_code = sb.tile([P, S], U32, name="x_code", tag="scale_then_code", align_bytes=64)
+        y = [ps.tile([P, S], F32, name="y%d" % a) for a in range(TILES)]
+        HALF = S // 2
+        for h in range(2):
+            nc.vector.tensor_copy(x_code[:, h * HALF:(h + 1) * HALF], word_table[:].bitcast(U32).indirect(offsets[:, h * HALF // 16:(h + 1) * HALF // 16]))
+        for a in range(TILES):
+            for h in range(2):
+                cols = slice(h * HALF, (h + 1) * HALF)
+                rows = slice(a * P, (a + 1) * P)
+                nc.tensor.matmul_mx(out=y[a][:, cols], lhsT=h_code[:, rows].bitcast(FP8X4), lhsT_scale=h_scale[:, rows],
+                                    rhs=x_code[:, cols].bitcast(FP8X4), rhs_scale=x_scale[:, cols], start=True, stop=True)
+
+        def col(name):
+            return [sb.tile([P, 1], F32, name="%s%d" % (name, a)) for a in range(TILES)]
+
+        def full(name):
+            return [sb.tile([P, S], F32, name="%s%d" % (name, a)) for a in range(TILES)]
+
+        neg_max, z, rz, sc, nrz = col("neg_max"), col("z"), col("rz"), col("sc"), col("nrz")
+        s1, s2, s3, c1, c2, c3 = col("s1"), col("s2"), col("s3"), col("c1"), col("c2"), col("c3")
+        e, q1, q2, q3, r1, r2, r3 = full("e"), full("q1"), full("q2"), full("q3"), full("r1"), full("r2"), full("r3")
+        tiles = range(TILES)
+        for a in tiles:
+            nc.vector.tensor_reduce(neg_max[a][:], y[a][:], AX.X, ALU.max, negate=True)
+            nc.scalar.activation(e[a][:], y[a][:], ACT.Exp, bias=neg_max[a][:], scale=1.0, accum_out=z[a][:])
+        for a in tiles:
+            nc.vector.scalar_tensor_tensor(r1[a][:], g_sb[0][:, a, :], -1.0, e[a][:], ALU.mult, ALU.mult, accum_out=s1[a][:])
+            nc.vector.reciprocal(rz[a][:], z[a][:])
+            nc.scalar.activation(c1[a][:], s1[a][:], ACT.Copy, bias=1.0, scale=rz[a][:])
+            nc.scalar.activation(sc[a][:], rz[a][:], ACT.Copy, scale=OUT_SCALE)
+            nc.scalar.activation(nrz[a][:], rz[a][:], ACT.Copy, scale=-1.0)
+        for a in tiles:
+            nc.vector.scalar_tensor_tensor(q1[a][:], g_sb[0][:, a, :], c1[a][:], e[a][:], ALU.add, ALU.mult)
+        for a in tiles:
+            nc.vector.scalar_tensor_tensor(r2[a][:], g_sb[1][:, a, :], sc[a][:], q1[a][:], ALU.mult, ALU.mult, accum_out=s2[a][:])
+            nc.scalar.activation(c2[a][:], s2[a][:], ACT.Identity, bias=sc[a][:], scale=nrz[a][:])
+        for a in tiles:
+            nc.vector.scalar_tensor_tensor(q2[a][:], q1[a][:], c2[a][:], r2[a][:], ALU.mult, ALU.add)
+        for a in tiles:
+            nc.vector.scalar_tensor_tensor(r3[a][:], g_sb[2][:, a, :], -1.0 / OUT_SCALE, q2[a][:], ALU.mult, ALU.mult, accum_out=s3[a][:])
+            nc.scalar.activation(c3[a][:], s3[a][:], ACT.Copy, bias=1.0, scale=1.0)
+        for a in tiles:
+            nc.vector.scalar_tensor_tensor(q3[a][:], g_sb[2][:, a, :], c3[a][:], q2[a][:], ALU.add, ALU.mult)
+            nc.sync.dma_start(out[a * P:(a + 1) * P, :], q3[a][:])

@@ -29,21 +29,21 @@ def tile_picked_ysynth_three_p_kernel(tc, x_words, x_scales, hT, g1, g2, g3, off
         ps = ctx.enter_context(tc.psum_pool(name="ps", bufs=1))
 
         offsets = sb.tile([P, S // 16], U16, name="offsets")
-        word_table = sb.tile([P, T], I32, name="word_table", align_bytes=64)
         scale_table = sb.tile([P, T], U8, name="scale_table", tag="scale_then_code", align_bytes=64)
         h_raw = sb.tile([P, PACK, V], F32, name="h_raw")
-        warm = sb.tile([P, 1], F32, name="warm", tag="warm_then_g")
-        warm_out = sb.tile([P, 1], F32, name="warm_out")
+        warm = sb.tile([P, 1], F32, name="warm", tag="warm_then_words", align_bytes=64)
+        warm_out = sb.tile([P, 1], F32, name="warm_out", tag="warm_then_g")
 
-        nc.vector.memset(scale_table[:].bitcast(I32), 0)
         nc.vector.memset(warm[:], 0.0)
+        nc.vector.memset(scale_table[:].bitcast(I32), 0)
+        nc.scalar.activation(warm_out[:], warm[:], ACT.Exp)
 
         nc.sync.dma_start(offsets[:], offs)
         nc.sync.dma_start(h_raw[:], hT.rearrange("(p j) t -> p j t", j=PACK))
-        nc.sync.dma_start(word_table[:], x_words[0].rearrange("p n t -> p (n t)").bitcast(I32))
         for q in range(4):
-            nc.scalar.dma_start(scale_table[32 * q:32 * q + 4, :].bitcast(I32), x_scales[0, 4 * q:4 * q + 4, :].bitcast(I32))
-        nc.scalar.activation(warm_out[:], warm[:], ACT.Exp)
+            nc.sync.dma_start(scale_table[32 * q:32 * q + 4, :].bitcast(I32), x_scales[0, 4 * q:4 * q + 4, :].bitcast(I32))
+        word_table = sb.tile([P, T], I32, name="word_table", tag="warm_then_words", align_bytes=64)
+        nc.sync.dma_start(word_table[:], x_words[0].rearrange("p n t -> p (n t)").bitcast(I32))
         g_all = sb.tile([P, 3, TILES, S], F32, name="g_all", tag="warm_then_g")
         g_sb = [g_all[:, r] for r in range(3)]
         for r, g in enumerate((g1, g2, g3)):
@@ -52,22 +52,22 @@ def tile_picked_ysynth_three_p_kernel(tc, x_words, x_scales, hT, g1, g2, g3, off
         x_scale = sb.tile([P, S], U8, name="x_scale", align_bytes=64)
         nc.vector.tensor_copy(x_scale[:], scale_table[:].indirect(offsets[:]))
 
-        h_bf = sb.tile([P, V * PACK], BF16, name="h_bf", align_bytes=64)
-        h_code = sb.tile([P, V], U32, name="h_code", align_bytes=64)
+        h_bf = sb.tile([P, V * PACK], BF16, name="h_bf", tag="bf16_then_code", align_bytes=64)
+        h_code = sb.tile([P, V], U32, name="h_code", tag="scale_then_code", align_bytes=64)
         h_scale = sb.tile([P, V], U8, name="h_scale", align_bytes=64)
         nc.scalar.copy(h_bf[:].rearrange("p (c i j) -> p c j i", i=4, j=PACK), h_raw[:].rearrange("p j (c i) -> p c j i", i=4))
         nc.vector.quantize_mx(out=h_code[:].bitcast(FP8X4), scales=h_scale[:], in_=h_bf[:])
 
-        x_code = sb.tile([P, S], U32, name="x_code", tag="scale_then_code", align_bytes=64)
-        y = [ps.tile([P, S], F32, name="y%d" % a) for a in range(TILES)]
+        x_code = sb.tile([P, S], U32, name="x_code", tag="bf16_then_code", align_bytes=64)
         HALF = S // 2
+        y = [[ps.tile([P, HALF], F32, name="y%d_%d" % (a, h)) for h in range(2)] for a in range(TILES)]
         for h in range(2):
             nc.vector.tensor_copy(x_code[:, h * HALF:(h + 1) * HALF], word_table[:].bitcast(U32).indirect(offsets[:, h * HALF // 16:(h + 1) * HALF // 16]))
-        for a in range(TILES):
-            for h in range(2):
+        for h in range(2):
+            for a in range(TILES):
                 cols = slice(h * HALF, (h + 1) * HALF)
                 rows = slice(a * P, (a + 1) * P)
-                nc.tensor.matmul_mx(out=y[a][:, cols], lhsT=h_code[:, rows].bitcast(FP8X4), lhsT_scale=h_scale[:, rows],
+                nc.tensor.matmul_mx(out=y[a][h][:], lhsT=h_code[:, rows].bitcast(FP8X4), lhsT_scale=h_scale[:, rows],
                                     rhs=x_code[:, cols].bitcast(FP8X4), rhs_scale=x_scale[:, cols], start=True, stop=True)
 
         def col(name):
@@ -80,9 +80,12 @@ def tile_picked_ysynth_three_p_kernel(tc, x_words, x_scales, hT, g1, g2, g3, off
         s1, s2, s3, c1, c2, c3 = col("s1"), col("s2"), col("s3"), col("c1"), col("c2"), col("c3")
         e, q1, q2, q3, r1, r2, r3 = full("e"), full("q1"), full("q2"), full("q3"), full("r1"), full("r2"), full("r3")
         tiles = range(TILES)
+        neg_y, part = full("neg_y"), col("part")
         for a in tiles:
-            nc.vector.tensor_reduce(neg_max[a][:], y[a][:], AX.X, ALU.max, negate=True)
-            nc.scalar.activation(e[a][:], y[a][:], ACT.Exp, bias=neg_max[a][:], scale=1.0, accum_out=z[a][:])
+            nc.vector.tensor_scalar(neg_y[a][:, :HALF], y[a][0][:], -1.0, None, ALU.mult, ALU.min, accum_out=part[a][:])
+        for a in tiles:
+            nc.vector.tensor_scalar(neg_y[a][:, HALF:], y[a][1][:], -1.0, part[a][:], ALU.mult, ALU.min, accum_out=neg_max[a][:])
+            nc.scalar.activation(e[a][:], neg_y[a][:], ACT.Exp, bias=neg_max[a][:], scale=-1.0, accum_out=z[a][:])
         for a in tiles:
             nc.vector.scalar_tensor_tensor(r1[a][:], g_sb[0][:, a, :], -1.0, e[a][:], ALU.mult, ALU.mult, accum_out=s1[a][:])
             nc.vector.reciprocal(rz[a][:], z[a][:])
@@ -100,5 +103,7 @@ def tile_picked_ysynth_three_p_kernel(tc, x_words, x_scales, hT, g1, g2, g3, off
             nc.vector.scalar_tensor_tensor(r3[a][:], g_sb[2][:, a, :], -1.0 / OUT_SCALE, q2[a][:], ALU.mult, ALU.mult, accum_out=s3[a][:])
             nc.scalar.activation(c3[a][:], s3[a][:], ACT.Copy, bias=1.0, scale=1.0)
         for a in tiles:
-            nc.vector.scalar_tensor_tensor(q3[a][:], g_sb[2][:, a, :], c3[a][:], q2[a][:], ALU.add, ALU.mult)
-            nc.sync.dma_start(out[a * P:(a + 1) * P, :], q3[a][:])
+            for h in range(2):
+                cols = slice(h * HALF, (h + 1) * HALF)
+                nc.vector.scalar_tensor_tensor(q3[a][:, cols], g_sb[2][:, a, cols], c3[a][:], q2[a][:, cols], ALU.add, ALU.mult)
+                (nc.sync if h == 0 else nc.scalar).dma_start(out[a * P:(a + 1) * P, cols], q3[a][:, cols])

from contextlib import ExitStack

import concourse.mybir as mybir

K, T, S, V = 512, 2048, 512, 256
FLOPS = 2 * K * S * V

F32 = mybir.dt.float32
BF16 = mybir.dt.bfloat16
I32 = mybir.dt.int32
U32 = mybir.dt.uint32
U16 = mybir.dt.uint16
U8 = mybir.dt.uint8
FP8X4 = mybir.dt.float8_e4m3fn_x4
ALU = mybir.AluOpType
ACT = mybir.ActivationFunctionType
AX = mybir.AxisListType

P = 128
PACK = 4
TILES = V // P
OUT_SCALE = 512.0


def tile_picked_ysynth_three_p_kernel(tc, x_words, x_scales, hT, g1, g2, g3, offs, out):
    nc = tc.nc
    with ExitStack() as ctx:
        sb = ctx.enter_context(tc.tile_pool(name="sb", bufs=1))
        ps = ctx.enter_context(tc.psum_pool(name="ps", bufs=1))

        offsets = sb.tile([P, S // 16], U16, name="offsets")
        scale_table = sb.tile([P, T], U8, name="scale_table", tag="scale_then_code", align_bytes=64)
        h_raw = sb.tile([P, PACK, V], F32, name="h_raw")
        warm = sb.tile([P, 1], F32, name="warm", tag="warm_then_words", align_bytes=64)
        warm_out = sb.tile([P, 1], F32, name="warm_out", tag="warm_then_g")

        nc.vector.memset(warm[:], 0.0)
        nc.vector.memset(scale_table[:].bitcast(I32), 0)
        nc.scalar.activation(warm_out[:], warm[:], ACT.Exp)

        nc.sync.dma_start(offsets[:], offs)
        nc.sync.dma_start(h_raw[:], hT.rearrange("(p j) t -> p j t", j=PACK))
        for q in range(4):
            nc.sync.dma_start(scale_table[32 * q:32 * q + 4, :].bitcast(I32), x_scales[0, 4 * q:4 * q + 4, :].bitcast(I32))
        word_table = sb.tile([P, T], I32, name="word_table", tag="warm_then_words", align_bytes=64)
        nc.sync.dma_start(word_table[:], x_words[0].rearrange("p n t -> p (n t)").bitcast(I32))
        g_all = sb.tile([P, 3, TILES, S], F32, name="g_all", tag="warm_then_g")
        g_sb = [g_all[:, r] for r in range(3)]
        for r, g in enumerate((g1, g2, g3)):
            nc.sync.dma_start(g_sb[r], g.rearrange("(a p) s -> p a s", p=P))

        x_scale = sb.tile([P, S], U8, name="x_scale", align_bytes=64)
        nc.vector.tensor_copy(x_scale[:], scale_table[:].indirect(offsets[:]))

        h_bf = sb.tile([P, V * PACK], BF16, name="h_bf", tag="bf16_then_code", align_bytes=64)
        h_code = sb.tile([P, V], U32, name="h_code", tag="scale_then_code", align_bytes=64)
        h_scale = sb.tile([P, V], U8, name="h_scale", align_bytes=64)
        nc.scalar.copy(h_bf[:].rearrange("p (c i j) -> p c j i", i=4, j=PACK), h_raw[:].rearrange("p j (c i) -> p c j i", i=4))
        nc.vector.quantize_mx(out=h_code[:].bitcast(FP8X4), scales=h_scale[:], in_=h_bf[:])

        x_code = sb.tile([P, S], U32, name="x_code", tag="bf16_then_code", align_bytes=64)
        HALF = S // 2
        y = [[ps.tile([P, HALF], F32, name="y%d_%d" % (a, h)) for h in range(2)] for a in range(TILES)]
        for h in range(2):
            nc.vector.tensor_copy(x_code[:, h * HALF:(h + 1) * HALF], word_table[:].bitcast(U32).indirect(offsets[:, h * HALF // 16:(h + 1) * HALF // 16]))
        for h in range(2):
            for a in range(TILES):
                cols = slice(h * HALF, (h + 1) * HALF)
                rows = slice(a * P, (a + 1) * P)
                nc.tensor.matmul_mx(out=y[a][h][:], lhsT=h_code[:, rows].bitcast(FP8X4), lhsT_scale=h_scale[:, rows],
                                    rhs=x_code[:, cols].bitcast(FP8X4), rhs_scale=x_scale[:, cols], start=True, stop=True)

        def col(name):
            return [sb.tile([P, 1], F32, name="%s%d" % (name, a)) for a in range(TILES)]

        def full(name):
            return [sb.tile([P, S], F32, name="%s%d" % (name, a)) for a in range(TILES)]

        neg_max, z, rz, sc, nrz = col("neg_max"), col("z"), col("rz"), col("sc"), col("nrz")
        s1, s2, s3, c1, c2, c3 = col("s1"), col("s2"), col("s3"), col("c1"), col("c2"), col("c3")
        e, q1, q2, q3, r1, r2, r3 = full("e"), full("q1"), full("q2"), full("q3"), full("r1"), full("r2"), full("r3")
        tiles = range(TILES)
        neg_y, part = full("neg_y"), col("part")
        for a in tiles:
            nc.vector.tensor_scalar(neg_y[a][:, :HALF], y[a][0][:], -1.0, None, ALU.mult, ALU.min, accum_out=part[a][:])
        for a in tiles:
            nc.vector.tensor_scalar(neg_y[a][:, HALF:], y[a][1][:], -1.0, part[a][:], ALU.mult, ALU.min, accum_out=neg_max[a][:])
            nc.scalar.activation(e[a][:], neg_y[a][:], ACT.Exp, bias=neg_max[a][:], scale=-1.0, accum_out=z[a][:])
        for a in tiles:
            nc.vector.scalar_tensor_tensor(r1[a][:], g_sb[0][:, a, :], -1.0, e[a][:], ALU.mult, ALU.mult, accum_out=s1[a][:])
            nc.vector.reciprocal(rz[a][:], z[a][:])
            nc.scalar.activation(c1[a][:], s1[a][:], ACT.Copy, bias=1.0, scale=rz[a][:])
            nc.scalar.activation(sc[a][:], rz[a][:], ACT.Copy, scale=OUT_SCALE)
            nc.scalar.activation(nrz[a][:], rz[a][:], ACT.Copy, scale=-1.0)
        for a in tiles:
            nc.vector.scalar_tensor_tensor(q1[a][:], g_sb[0][:, a, :], c1[a][:], e[a][:], ALU.add, ALU.mult)
        for a in tiles:
            nc.vector.scalar_tensor_tensor(r2[a][:], g_sb[1][:, a, :], sc[a][:], q1[a][:], ALU.mult, ALU.mult, accum_out=s2[a][:])
            nc.scalar.activation(c2[a][:], s2[a][:], ACT.Identity, bias=sc[a][:], scale=nrz[a][:])
        for a in tiles:
            nc.vector.scalar_tensor_tensor(q2[a][:], q1[a][:], c2[a][:], r2[a][:], ALU.mult, ALU.add)
        for a in tiles:
            nc.vector.scalar_tensor_tensor(r3[a][:], g_sb[2][:, a, :], -1.0 / OUT_SCALE, q2[a][:], ALU.mult, ALU.mult, accum_out=s3[a][:])
            nc.scalar.activation(c3[a][:], s3[a][:], ACT.Copy, bias=1.0, scale=1.0)
        for a in tiles:
            for h in range(2):
                cols = slice(h * HALF, (h + 1) * HALF)
                nc.vector.scalar_tensor_tensor(q3[a][:, cols], g_sb[2][:, a, cols], c3[a][:], q2[a][:, cols], ALU.add, ALU.mult)
                (nc.sync if h == 0 else nc.scalar).dma_start(out[a * P:(a + 1) * P, cols], q3[a][:, cols])
